import numpy as np, ml_dtypes
CORES = [9,25,41,57]
N = 4
BF = ml_dtypes.bfloat16
def gentries(a):
    return np.ascontiguousarray(a.reshape(8, 16, -1).transpose(0, 2, 1)).reshape(8, -1)
def gtable(e):
    e = np.asarray(e); return np.ascontiguousarray(e.reshape(8, -1, 16).transpose(0, 2, 1)).reshape(128, -1).astype(np.int32)
V, G, L, D, RO = 3584, 64, 768, 5, 3
S = (N - 1) * G; W = V + S
def weave(rng, share, ring=0.03, ends=False, most=V):
    o = rng.permutation(V); b = rng.random(V) < share; b[0] = True
    if ends: o = np.concatenate([np.array([0, V - 1]), rng.permutation(np.arange(1, V - 1))]); b[1:4] = True
    st = np.flatnonzero(b); en = np.append(st[1:], V) - 1; T = len(st); top = o[st]; last = o[en]
    par = np.empty(V, np.int64); side = np.zeros(V, np.int64); kd = np.full(V, W, np.int64)
    par[o[1:]] = o[:-1]
    w = rng.permutation(T); gp = rng.permutation(S); n = min((T + 1) // 2, int(rng.integers(S // 2, S + 1)), most)
    if ends: w = np.concatenate([np.array([0, 1]), 2 + rng.permutation(T - 2)]); gp = np.concatenate([np.array([0, S - 1]), 1 + rng.permutation(S - 2)])
    par[top[w[:n]]] = V + gp[:n]; side[top[w[:n]]] = rng.integers(0, 2, n)
    c = w[n:]; z = rng.random(len(c)) < ring
    par[top[c[z]]] = last[c[z]]
    e = c[~z]; v = rng.permutation(V)
    if ends:
        for i in range(min(4, len(e))):
            j = int(np.flatnonzero(v == top[e[i]])[0]); h = v[i]; v[i] = v[j]; v[j] = h
    v = v[:len(e)]; par[top[e]] = v; side[top[e]] = 1; kd[v] = top[e]
    return par, side, kd
def pairs(rng, share, coin, classes=False):
    h = V // 2; o = rng.permutation(V)
    if classes: o = o[np.argsort(-((o - int(rng.integers(0, 16))) % 16), kind="stable")]; o[:h] = rng.permutation(o[:h])
    a, f = o[:h], o[h:]; b = rng.random(h) < share; b[0] = True
    st = np.flatnonzero(b); en = np.append(st[1:], h) - 1; T = len(st)
    par = np.empty(V, np.int64); side = np.zeros(V, np.int64); kd = np.full(V, W, np.int64)
    par[a[1:]] = a[:-1]; par[f] = a
    mid = np.ones(h, bool); mid[en] = False; j = np.flatnonzero(mid); c = rng.random(len(j)) < coin
    side[f[j]] = np.where(c, 0, 1); side[a[j + 1]] = np.where(c, 1, 0); kd[a[j]] = np.where(c, a[j + 1], f[j])
    w = rng.permutation(T); n = min((T + 1) // 2, int(rng.integers(S // 2, S + 1))); top = a[st]
    side[top] = 1; par[top[w[:n]]] = V + rng.permutation(S)[:n]; side[top[w[:n]]] = rng.integers(0, 2, n)
    e = a[en][rng.permutation(T)[:T - n]]; par[top[w[n:]]] = e; kd[e] = top[w[n:]]
    return par, side, kd, a, f
def comb(rng, T):
    R = 8; m = min(D, 5); n = T - R; q = V - R * m; big = min(n, (q - 2 * n) // (D - 2)); rest = q - 2 * n - big * (D - 2)
    ln = np.full(n, 2, np.int64); ln[:big] = D
    if big < n: ln[big] += rest; rest = 0
    ln = np.concatenate([np.full(R, m, np.int64), rng.permutation(ln), np.ones(rest, np.int64)])
    o = rng.permutation(V); en = np.add.accumulate(ln) - 1; top = o[en - ln + 1]; last = o[en]
    par = np.empty(V, np.int64); side = np.zeros(V, np.int64); kd = np.full(V, W, np.int64)
    par[o[1:]] = o[:-1]
    free = np.ones(V, bool); free[o[:R * m]] = False; free[last[:T]] = False; a = rng.permutation(np.flatnonzero(free))
    par[top[:R]] = last[:R]; side[top[:R]] = 1; kd[last[:R]] = top[:R]
    t = rng.permutation(top[R:]); w = int(rng.integers(S // 2, S + 1))
    par[t[:w]] = V + rng.permutation(S)[:w]; side[t[:w]] = rng.integers(0, 2, w)
    e = t[w:]; v = a[:len(e)]; par[e] = v; side[e] = 1; kd[v] = e
    off = np.zeros(V, np.int64); off[last[:T]] = 4
    for k in range(1, m): off[o[en[:R] - k]] = max(0, 4 - (m - k))
    sg = np.empty((16, V), np.int64); sg[:, o] = np.repeat(2 * rng.integers(0, 2, (16, len(ln))) - 1, ln, axis=1)
    return par, side, kd, a, np.where(free[None, :], rng.integers(0, 2, (16, V)), sg * off[None, :])
def knit(z):
    return [np.stack([np.stack([z[q][g][i] for g in range(8)]) for q in range(N)]) for i in range(3)]
def shown(rng):
    return np.ascontiguousarray(np.argsort(rng.random((N, 8, V)), axis=-1)[..., :S]).reshape(N, 8, N - 1, G)
def seen(x, sl):
    z = []
    for r in range(N):
        w = [x[r]]
        for d in range(1, N):
            q = (r - d) % N; w.append(np.take_along_axis(x[q], sl[q][:, d - 1][:, None, :], 2))
        z.append(np.concatenate(w, axis=2))
    return np.stack(z)
def gaps(full, par):
    return np.add.reduce(np.abs(full[..., :V] - np.take_along_axis(full, par[:, :, None, :], 3)), axis=2)
def level(v, share):
    s = np.sort(v, axis=-1); n = v.shape[-1]; i = np.clip(((1 - share) * n).astype(np.int64), 0, n - 1)
    return np.take_along_axis(s, i[..., None], 2)[..., 0]
def numbers16(rng):
    u = rng.random((N, 8, 16, V)) ** np.exp2(rng.integers(-1, 2, (N, 8, 1, V)))
    return np.minimum(np.floor(16 * u), 15).astype(np.int64)
def pack(x, par, side, kd, sl, th, A):
    return {"x": np.ascontiguousarray(x.reshape(N, 128, V)).astype(np.float32).astype(BF), "hang": np.stack([gtable(a) for a in 2 * par + side]), "kid": np.stack([gtable(a) for a in kd]),
            "shw": np.stack([gtable(a.reshape(8, -1)) for a in sl]), "bar": np.repeat(np.stack([th, A], axis=-1), 16, axis=1).astype(np.int32)}
def setup_inputs(rng):
    sh = rng.choice(np.array([0.15, 0.25, 0.4]), (N, 8))
    par, side, kd = knit([[weave(rng, sh[q, g]) for g in range(8)] for q in range(N)]); sl = shown(rng); x = numbers16(rng)
    th = level(gaps(seen(x, sl), par), rng.choice(np.array([0.1, 0.2, 0.35, 0.6]), (N, 8)))
    A = level(np.add.reduce(x, axis=2), rng.choice(np.array([0.02, 0.08, 0.2]), (N, 8)))
    return pack(x, par, side, kd, sl, th, A)
def setup_inputs_room(rng):
    h = V // 2; b = rng.integers(4, 12, (8, 16, 1)); th = rng.integers(8, 41, (N, 8))
    A = np.add.reduce(b[:, :, 0], axis=1)[None, :] + rng.choice(np.array([0, 1, 1, 16]), (N, 8))
    x = np.empty((N, 8, 16, V), np.int64); sl = np.empty((N, 8, N - 1, G), np.int64); z = []
    for q in range(N):
        z.append([])
        for g in range(8):
            k = pairs(rng, 0.3, 0.5, g > 5); z[q].append(k); a, f = k[3], k[4]
            sl[q, g] = rng.permutation(a)[:S].reshape(N - 1, G)
            n = int(rng.choice(np.array([0, 1, L - 1, L, L + 1, h])))
            if q < 2: n = (L, L + 1, h, L - 1, 1, 0, L, L + 1)[(g + q) % 8]
            t0 = int(th[q, g]); coin = rng.random(h) < 0.5; hit = (np.arange(h) if g > 5 else rng.permutation(h)) < n
            t = np.where(hit, np.where(coin, t0, rng.integers(t0, 64, h)), np.where(coin, t0 - 1, rng.integers(0, t0, h)))
            size = (t[None, :] + (np.arange(16)[:, None] + rng.integers(0, 16, h)[None, :]) % 16) // 16
            v = np.repeat(b[g], V, axis=1); v[:, f] = b[g] + size * (2 * rng.integers(0, 2, (16, h)) - 1); x[q, g] = v
    par, side, kd = knit(z)
    return pack(x, par, side, kd, sl, th, A)
def setup_inputs_deep(rng):
    few = min(L, -(-V // D)); z = []
    for q in range(N): z.append([weave(rng, 0.04, 0.3) if g % 4 == 0 else pairs(rng, 0.02, 0.0) if g % 4 == 1 else comb(rng, L if g % 4 == 2 else few) for g in range(8)])
    par, side, kd = knit(z); sl = shown(rng); x = numbers16(rng); b = rng.integers(4, 12, (8, 16, 1))
    for q in range(N):
        for g in (2, 3, 6, 7):
            x[q, g] = b[g] + z[q][g][4]; sl[q, g] = rng.permutation(z[q][g][3])[:S].reshape(N - 1, G)
    th = level(gaps(seen(x, sl), par), rng.choice(np.array([0.03, 0.06, 0.1]), (N, 8)))
    th[:, np.array([2, 3, 6, 7])] = rng.integers(17, 49, (N, 4))
    return pack(x, par, side, kd, sl, th, np.full((N, 8), 255))
def setup_inputs_ends(rng):
    par, side, kd = knit([[weave(rng, 0.3, 0.2, True) for g in range(8)] for q in range(N)]); sl = np.empty((N, 8, N - 1, G), np.int64)
    for q in range(N):
        for g in range(8): sl[q, g] = np.concatenate([np.array([0]), rng.permutation(np.arange(1, V - 1))[:S - 2], np.array([V - 1])]).reshape(N - 1, G)
    x = np.repeat(15 * rng.integers(0, 2, (N, 8, 1, V)), 16, axis=2)
    odd = (rng.random((N, 8, 1, V)) < 0.3) & (np.arange(16)[:, None] == rng.integers(0, 16, (N, 8, 1, V)))
    x = np.where(odd, np.abs(x - 1), x)
    th = rng.choice(np.array([0, 1, 239, 240, 241]), (N, 8)); A = rng.choice(np.array([0, 1, 239, 240, 241, 255]), (N, 8))
    th[0] = np.array([0, 1, 239, 240, 240, 0, 239, 1]); A[0] = np.array([241, 240, 239, 241, 0, 1, 241, 240])
    return pack(x, par, side, kd, sl, th, A)
def setup_inputs_afar(rng):
    sh = rng.choice(np.array([0.2, 0.3, 0.4]), (N, 8))
    par, side, kd = knit([[weave(rng, sh[q, g]) for g in range(8)] for q in range(N)]); sl = shown(rng)
    for q in range(N):
        sl[q, 1] = ((V // 16) * int(rng.integers(0, 9)) + rng.permutation(S)).reshape(N - 1, G)
        v = np.argsort((np.arange(V) - int(rng.integers(0, 16))) % 16, kind="stable")[:S]; sl[q, 4] = rng.permutation(v).reshape(N - 1, G)
    b = np.empty((N, 8, 16, 1), np.int64)
    for g in range(8):
        o = rng.permutation(16)
        for q in range(N): b[q, g, :, 0] = [13 if bin(int(i) & (q + 1)).count("1") % 2 else 2 for i in o]
    x = b + rng.integers(0, 2, (N, 8, 16, V))
    th = rng.choice(np.array([17, 40, 80, 90]), (N, 8)); th[rng.integers(0, N, 8), np.arange(8)] = rng.integers(242, 256, 8)
    return pack(x, par, side, kd, sl, th, rng.choice(np.array([128, 255, 255]), (N, 8)))
def setup_inputs_spread(rng):
    sh = 0.02 + 0.6 * rng.random((N, 8)); full = np.arange(8) % 3 == 2
    par, side, kd = knit([[weave(rng, 0.9, 0.0, False, 16) if full[g] else weave(rng, sh[q, g], 0.1) for g in range(8)] for q in range(N)]); sl = shown(rng)
    x = np.minimum(np.floor(np.exp2(4 * rng.random((N, 8, 1, V))) * (0.05 + rng.random((N, 8, 16, V)))), 15).astype(np.int64)
    th = level(gaps(seen(x, sl), par), np.where(full, 0.15, np.exp2(-6 * rng.random((N, 8)))))
    A = np.where((rng.random((N, 8)) < 0.7) | full, level(np.add.reduce(x, axis=2), np.where(full, 0.03, np.exp2(-6 * rng.random((N, 8))))), rng.integers(0, 256, (N, 8)))
    return pack(x, par, side, kd, sl, th, A)
def check_inputs(d):
    bad = []; x = np.asarray(d["x"]).astype(np.float32)
    if not np.all((x >= 0) & (x <= 15) & (x == np.floor(x))): bad.append("range of x")
    for k, lo, hi in (("hang", 0, 2 * W - 1), ("kid", 0, W), ("shw", 0, V - 1), ("bar", 0, 255)):
        if np.min(d[k]) < lo or np.max(d[k]) > hi: bad.append("range of " + k)
    b = np.asarray(d["bar"]).reshape(N, 8, 16, 2)
    if np.any(b != b[:, :, :1]): bad.append("bar not alike on a group's rows")
    if bad: return bad
    for r in range(N):
        hs, ks, ss = (gentries(np.asarray(d[k][r])).astype(np.int64) for k in ("hang", "kid", "shw"))
        for g in range(8):
            h = hs[g]; p = h >> 1; own = p < V
            if len(np.unique(h[own])) < np.count_nonzero(own): bad.append("two stitches on one side of a parent")
            if len(np.unique(p[~own])) < np.count_nonzero(~own): bad.append("two stitches under one ghost")
            m = np.flatnonzero(own & (h % 2 == 1)); want = np.full(V, W, np.int64); want[p[m]] = m
            if np.any(ks[g] != want): bad.append("kid against hang")
            if len(np.unique(ss[g])) < S: bad.append("a stitch shown twice")
    return sorted(set(bad))
def reference(x, hang, kid, shw, bar):
    now = x.astype(np.float32).astype(np.int64).reshape(N, 8, 16, V)
    h = np.stack([gentries(a) for a in hang]).astype(np.int64); par = h >> 1; side = h & 1
    kd = np.stack([gentries(a) for a in kid]).astype(np.int64); sl = np.stack([gentries(a) for a in shw]).astype(np.int64).reshape(N, 8, N - 1, G)
    th = bar[:, ::16, 0].astype(np.int64); A = bar[:, ::16, 1].astype(np.int64)
    flag = np.zeros((N, 8, V), bool)
    for rnd in range(RO):
        full = seen(now, sl)
        cand = (gaps(full, par) >= th[:, :, None]) | flag
        drop = cand & (np.add.accumulate(cand.astype(np.int64), axis=2) <= L)
        stop = np.ones((N, 8, W), bool); stop[..., :V] = drop | (np.add.reduce(now, axis=2) >= A[:, :, None])
        slot = np.zeros((N, 8, W), bool); now = now.copy(); par2 = par.copy(); side2 = side.copy(); kd2 = kd.copy()
        for r in range(N):
            for g in range(8):
                p, s, c1, st, f = par[r, g], side[r, g], kd[r, g], stop[r, g], full[r, g]
                p2, s2, c2, new = par2[r, g], side2[r, g], kd2[r, g], now[r, g]
                d = [np.flatnonzero(drop[r, g])]; live = [np.ones(len(d[0]), bool)]
                top = np.full(len(d[0]), W, np.int64)
                for k in range(D):
                    i = np.flatnonzero(live[k]); v = d[k][i]; u = p[v]
                    nxt = d[k].copy(); nxt[i] = u; go = np.zeros(len(nxt), bool); go[i] = (s[v] == 0) & ~st[u]
                    top[i] = c1[v]; d.append(nxt); live.append(go)
                anchor = d[D]; slot[r, g][anchor[anchor >= V]] = True
                up = f[:, anchor]
                for k in range(D - 1, -1, -1):
                    up = (f[:, d[k]] + up) >> 1
                    new[:, d[k][live[k]]] = up[:, live[k]]
                for k in range(D):
                    i = np.flatnonzero(live[k]); v = d[k][i]
                    if k == 0:
                        c = top[i]; has = c < V; c2[v] = c; p2[c[has]] = v[has]; s2[c[has]] = 1
                    else:
                        w = d[k - 1][i]; c = c1[w]; has = c < V
                        c2[v] = np.where(has, w, W); p2[c[has]] = v[has]; s2[c[has]] = 0; s2[w[has]] = 1
        par, side, kd = par2, side2, kd2
        flag = np.zeros((N, 8, V), bool)
        for q in range(N):
            for e in range(1, N):
                r = (q + e) % N; z = slot[r, :, V + (e - 1) * G:V + e * G]
                for g in range(8): flag[q, g][sl[q, g, e - 1][z[g]]] = True
    return {"y": now.reshape(N, 128, V).astype(np.float32).astype(BF), "yh": (2 * par + side).astype(np.float32)}

import numpy as np
from concourse.bass import DstId, RemoteDMATransfer
from concourse.mybir import AluOpType as ALU, ActivationFunctionType as AF

N, V, G, L, RO = 4, 3584, 64, 768, 3
W = V + (N - 1) * G
TR = W + 16
UB = TR
XW = UB + 5 * L
BW = W + TR + L
M = 4096.0
bf, f32, i32, u16 = "bfloat16", "float32", "int32", "uint16"
AH, AL, CH, CL, NT, FL, EH, EL, EE, DH, DL, HS, AC, SH, SL, RG = range(16)
B_PAR, B_IDX, B_YH, B_OFF, B_ANC, B_SRC, B_FLP, B_SUM = range(8)
M_G, M_H, M_R, M_C, M_M, M_F, M_I, M_HALF, M_ONE, M_TRI, M_STRI, M_END = range(12)

SCRATCH = {}


def _sb(name, cols, dtp):
    SCRATCH[name] = ("sbuf", [128] + list(cols), dtp)


for _r in range(RO):
    _sb("X%d" % _r, [XW], bf)
    _sb("B%d" % _r, [BW], bf)
for _r in range(1, RO):
    _sb("MS%d" % _r, [384], bf)
    _sb("LD%d" % _r, [384], bf)
for _n, _c, _d in [
    ("MS0", 192, bf), ("PF", V, bf), ("XC", V, bf), ("DD", V, bf), ("AB", V, bf), ("SC", 5 * L, bf), ("CT", V + 224, bf),
    ("GK", 5 * L, bf), ("RC", 6 * L, bf), ("NG", 6 * L, bf), ("CW", L, bf), ("CM", L, bf), ("SQ", 384, bf), ("EG", 192, bf),
    ("LM", 12 * 128, bf), ("ZZ", 464, bf), ("cw", 224, bf), ("cb", 32, bf), ("CC", 224, bf), ("CS", 224, bf),
    ("iv", 48, bf), ("DR", 224, bf), ("DT", 224, bf), ("HV", 224, bf), ("at", 4 * 224, bf), ("idg", 2 * 240, bf),
    ("sdg", 3 * 240, bf), ("one", 224, bf),
    ("jw", L, f32), ("RT", 224, f32), ("jl", 48, f32), ("vl", 224, f32), ("trm", 48, f32), ("trl", 48, f32), ("col", 16, f32),
    ("bias", 16, f32), ("barf", 4, f32), ("t0", 224, f32), ("t1", 48, f32),
    ("t5", 48, f32), ("t6", 16, f32), ("t7", 16, f32), ("t8", 48, f32), ("yo", 224, f32), ("t9", 48, f32),
    ("hg", 224, i32), ("kd", 224, i32), ("sw", 12, i32), ("br", 2, i32), ("n0", 240, i32), ("n1", 240, i32), ("n2", 240, i32),
    ("n3", 240, i32), ("n4", 240, i32), ("pi", 4, i32),
    ("go", 224, u16), ("ix", 224, u16), ("sr", 224, u16), ("se", 24, u16), ("fp", 12, u16), ("ss", 12, u16), ("co", 16, u16),
    ("cl", 48, u16), ("dk", 5 * 48, u16), ("of", 5 * 48, u16), ("an", 4 * 48, u16)]:
    _sb(_n, [_c], _d)
_sb("BS", [8, 144], bf)
_sb("SE", [16, 144], bf)
_sb("L3", [12 * 8, 16], bf)
for _k in range(8):
    SCRATCH["ps%d" % _k] = ("psum", [128, 512], f32)
NDMA = 48
SEMAPHORES = ["v", "a", "p", "g"] + ["ar%d" % r for r in range(RO)] + ["ls%d" % r for r in range(RO)] + ["d%d" % k for k in range(NDMA)]

CY, PC, GA, SA = 1.04, 0.52, 1.56, 3.8
SAME, CROSS = 40, 100
PASSES = 1500
BONUS = {0:54,1:77,2:31,3:27,4:31,5:15,6:105,7:2,9:9,11:8,13:31,14:10,16:120,18:1,20:66,23:55,24:11,26:47,27:28,28:117,30:11,31:6,32:39,33:5,36:36,37:3,39:68,40:20,41:72,42:1,43:30,44:73,45:32,46:20,47:15,49:58,50:242,51:9,52:36,53:12,54:77,55:166,56:73,58:89,60:1,66:15,68:5,70:2,72:70,74:8,76:29,77:3,78:2,82:32,84:10,86:4,89:58,90:10,91:65,92:27,96:16,97:36,98:114,99:65,100:1,101:38,102:76,103:33,104:4,105:35,106:35,107:31,108:12,112:2,113:60,114:69,115:165,116:4,117:19,119:16,120:17,121:22,122:86,126:31,127:122,128:4,129:19,130:45,132:37,133:14,135:12,136:35,137:106,138:35,139:2,140:54,146:5,148:3,149:2,151:5,155:11,156:12,158:14,159:77,160:57,161:81,165:92,166:2,167:23,168:6,169:12,171:40,172:1,174:7,175:33,176:1,178:5,179:17,183:6,184:3,185:4,186:20,188:51,189:2,190:45,191:31,194:23,199:1,202:28,203:24,210:2,211:12,218:34,222:12,223:15,224:20,225:5,226:8,227:17,231:3,232:2,233:1,234:13,235:58,236:4,237:1,238:9,239:17,242:5,243:248,244:13,246:6,250:44,251:10,255:2,256:3,258:3,259:13,260:6,261:2,264:12,265:2,269:49,270:25,271:6,272:12,275:24,277:20,282:7,283:18,284:1,286:11,289:29,291:176,292:3,293:106,294:68,295:53,314:127,315:23,316:33,318:60,319:115,322:30,323:3,324:6,325:11,326:30,327:36,328:35,329:181,330:95,331:117,332:119,334:4,336:81,337:6,338:29,339:65,340:61,341:31,342:39,343:1,344:19,347:127,348:2,351:4,353:8,355:54,356:7,358:21,359:25,362:2,365:4,366:37,371:5,373:20,374:1,378:37,379:5,382:6,387:49,390:45,392:60,393:15,395:1,396:12,397:12,398:24,401:22,403:2,408:19,410:25,412:8,417:17,422:117,428:18,429:4,430:1,431:16,432:106,433:12,436:1,437:6,438:21,439:5,441:20,448:17,449:2,451:47,453:5,454:8,456:3,461:4,462:25,463:5,464:2,467:26,477:15,478:3,479:15,480:6,482:7,484:31,485:5,486:11,487:12,488:24,489:6,490:46,491:44,492:19,493:4,495:3,500:5,508:5,513:2,514:1,516:9,517:27,519:18,521:20,523:2,530:14,532:9,533:2,535:10}
ALLP = (1 << 128) - 1
_ar = {}
_plan = {}


def vw(name, *idx, p=slice(None)):
    if name not in SCRATCH:
        return {"n": name, "i": None, "hbm": idx, "w": 0, "e": 0}
    shp = SCRATCH[name][1]
    if name not in _ar:
        _ar[name] = np.arange(int(np.prod(shp[1:]))).reshape(shp[1:])
    a = _ar[name][tuple(idx)] if idx else _ar[name]
    pm = ALLP if p == slice(None) else sum(1 << q for q in range(128)[p])
    w = 2 if SCRATCH[name][2] in (bf, u16) else 4
    return {"n": name, "i": (p,) + tuple(idx), "lo": int(a.min()), "hi": int(a.max()) + 1, "pm": pm, "e": int(a.size), "w": w}


def c(name, a=None, b=None, s=None, p=slice(None)):
    return vw(name, slice(a, b, s), p=p)


def ind(win, off):
    return {"ind": (win, off), "e": 16 * off["e"], "w": win["w"]}


def build(rank, T, topo):
    ops = []

    def ap(x):
        if not isinstance(x, dict):
            return x
        if "ind" in x:
            return ap(x["ind"][0]).indirect(ap(x["ind"][1]))
        if x["i"] is None:
            return T[x["n"]][x["hbm"]] if x["hbm"] else T[x["n"]][:]
        return T[x["n"]][x["i"]]

    def flat(xs, out=False):
        z = []
        for x in xs:
            if isinstance(x, dict):
                if "ind" in x:
                    z += [x["ind"][0]] if out else list(x["ind"])
                elif x["i"] is not None:
                    z.append(x)
        return z

    def add(alts, outs, ins, kind="c", **kw):
        rd = flat(ins) + [o["ind"][1] for o in outs if "ind" in o]
        ops.append(dict(alts=alts, w=flat(outs, True), r=rd, kind=kind, **kw))

    def vcost(out, ins, two=False):
        n = out["e"]
        if "ind" in out:
            return 50 + n * SA * CY
        if any(isinstance(x, dict) and "ind" in x for x in ins):
            return 50 + n * GA * CY
        big = [x for x in ins if isinstance(x, dict) and x["e"] > 1] + [out]
        f = 0.5 if all(x["w"] == 2 for x in big) else 1.0
        if two:
            f = 1.0 if any(x["n"].startswith("ps") for x in big[:-1]) else 2.0
        return 30 + max(64, n * f) * CY

    def acost(out, x):
        return 65 + max(64, out["e"] * (GA if "ind" in x else 1.0)) * CY

    def cp(out, x, eng="v"):
        al = {}
        if "v" in eng:
            al["v"] = (vcost(out, [x]), lambda g: g.vector.tensor_copy(ap(out), ap(x)))
        if "a" in eng:
            al["a"] = (acost(out, x), lambda g: g.scalar.activation(ap(out), ap(x), AF.Copy))
        if "g" in eng:
            al["g"] = (190 + 2 * out["e"] * CY, lambda g: g.affine_select(ap(out), ap(x), [[0, out["e"]]], ALU.is_ge, 0.0, 0, 1))
        add(al, [out], [x])

    def tt(out, a, b, op):
        add({"v": (vcost(out, [a, b], True), lambda g: g.vector.tensor_tensor(ap(out), ap(a), ap(b), op))}, [out], [a, b])

    def ts(out, a, s1, op0, s2=None, op1=None):
        if op1 is None:
            fn = lambda g: g.vector.tensor_scalar(ap(out), ap(a), ap(s1), None, op0)
        else:
            fn = lambda g: g.vector.tensor_scalar(ap(out), ap(a), ap(s1), ap(s2), op0, op1)
        add({"v": (vcost(out, [a]), fn)}, [out], [a, s1, s2])

    def addc(out, x, b, relu=False):
        if relu:
            fn = lambda g: g.vector.tensor_scalar(ap(out), ap(x), ap(b), 0.0, ALU.add, ALU.max)
        else:
            fn = lambda g: g.vector.tensor_scalar(ap(out), ap(x), ap(b), None, ALU.add)
        add({"v": (vcost(out, [x]), fn),
             "a": (acost(out, x), lambda g: g.scalar.activation(ap(out), ap(x), AF.Relu if relu else AF.Identity, bias=ap(b)))},
            [out], [x, b])

    def scan(out, a, b, op0, op1, init=0.0):
        add({"v": (vcost(out, [a, b]), lambda g: g.vector.tensor_tensor_scan(ap(out), ap(a), ap(b), ap(init), op0, op1))},
            [out], [a, b, init])

    def ms(out, val):
        add({"v": (vcost(out, []), lambda g: g.vector.memset(ap(out), val))}, [out], [])

    def mm(items, start=True, stop=True):
        def fn(g):
            z = None
            for k, (o, l, r) in enumerate(items):
                first = start and all(items[q][0] is not o for q in range(k))
                last = stop and all(items[q][0] is not o for q in range(k + 1, len(items)))
                z = g.tensor.matmul(ap(o), ap(l), ap(r), first, last)
            return z
        add({"p": (60 + sum(max(64, r["e"]) for o, l, r in items) * PC, fn)}, [o for o, l, r in items],
            [x for o, l, r in items for x in (l, r)])

    def base(b):
        return lambda i: vw("BS", b, slice(15 - i, 143 - i))

    def mat(m):
        return c("LM", 128 * m, 128 * m + 128)

    def tolist(out, bfn, name, a, n):
        return [(out, bfn(i), c(name, a + i, a + n, 16)) for i in range(16)]

    def tochunk(out, bfn, name, a, qs=range(16)):
        return [(out, bfn(q), c(name, a + 224 * q, a + 224 * q + 224)) for q in qs]

    def iota(out, pat, b, cm):
        if SCRATCH[out["n"]][2] == i32:
            fn = lambda g: g.iota(ap(out), pat, b, cm)
        else:
            fn = lambda g: g.iota(ap(out), pat, b, cm, allow_small_or_imprecise_dtypes=True)
        add({"g": (150 + 2 * out["e"] * CY, fn)}, [out], [])

    def asel(out, pat, op, fill, b, cm, src=None):
        src = src or out
        add({"g": (190 + 2 * out["e"] * CY, lambda g: g.affine_select(ap(out), ap(src), pat, op, fill, b, cm))}, [out], [src])

    def dma(out, x, nbytes):
        add({"s": (60, lambda g: g.sync.dma_start(ap(out), ap(x)))}, [out], [x], kind="dma", lat=2000 + nbytes / 180.0)

    def row(name, r, a, n):
        return c(name, a, a + n, p=slice(r, 128, 16))

    me = T.cores[rank]

    def exchange(r, src, land, width):
        eng = topo.engines(me, T.cores[(rank + 1) % N])
        h = len(eng) // 4
        sets = [eng[:2 * h], eng[2 * h:3 * h], eng[3 * h:4 * h]]

        def fn(g):
            tr = []
            for d in range(1, N):
                rid, pid, _ = topo.addr(T.cores[(rank + d) % N])
                tr.append(RemoteDMATransfer(dst_ids=[DstId(rid=rid, pnc=pid)], dma_engine_mask=sum(1 << e for e in sets[d - 1]),
                                            remote_sem=T.sem["ar%d" % r], src=ap(c(src, (d - 1) * width, d * width)),
                                            dst=ap(c(land[0], land[1] + (d - 1) * width, land[1] + d * width))))
            return g.remote_dma_fused(tr, local_sem=T.sem["ls%d" % r])
        add({"g": (1000, fn)}, [], [c(src, 0, 3 * width)], kind="send", lat=2500 if r else 5000, sem=("ls%d" % r, 4 * h))
        k = len(ops) - 1
        add({"n": (0, None)}, [c(land[0], land[1], land[1] + 3 * width)], [], kind="recv", lat=1000, sem=("ar%d" % r, 4 * h), after=[k])

    P = ["ps%d" % k for k in range(8)]
    PM, OHD, TOT = c("col", 0, 1), c("col", 1, 2), c("col", 2, 3)
    TH = c("barf", 0, 1)

    dma(c("sw"), vw("shw"), 6e3)
    dma(c("X0", 0, V), vw("x"), 917e3)
    dma(c("hg"), vw("hang"), 115e3)
    dma(c("kd"), vw("kid"), 115e3)
    dma(c("br"), vw("bar"), 1e3)
    cp(c("se", 0, 12), c("sw"))
    cp(c("MS0"), ind(c("X0", 0, V), c("se", 0, 12)))
    exchange(0, "MS0", ("X0", V), G)
    for a in range(0, V, 896):
        cp(c("XC", a, a + 896), c("X0", a, a + 896), "va")

    ms(vw("SE"), 0.0)
    ms(vw("BS"), 0.0)
    ms(vw("L3"), 0.0)
    asel(vw("SE", slice(None), slice(15, 143, 16)), [[-1, 16], [-16, 8]], ALU.not_equal, 1.0, 0, 1)

    def m3(m, a=0, b=16, s=None):
        return vw("L3", slice(8 * m, 8 * m + 8), slice(a, b, s))

    def ent(m, r, a, b, val, s=None, diag=False):
        o = m3(m, a, b, s)
        asel(o, [[-16, 8], [-1 if diag else 0, o["e"] // 8]], ALU.not_equal, val, -r, 1)

    ms(m3(M_ONE), 1.0)
    asel(m3(M_ONE), [[-16, 8], [0, 16]], ALU.is_ge, 0.0, 0, 1)
    asel(m3(M_ONE), [[16, 8], [0, 16]], ALU.is_ge, 0.0, 15, -1)
    asel(m3(M_TRI), [[16, 8], [1, 16]], ALU.is_ge, 0.0, 0, -1, src=m3(M_ONE))
    asel(m3(M_STRI), [[16, 8], [1, 16]], ALU.is_ge, 0.0, -1, -1, src=m3(M_ONE))
    ent(M_I, 0, 0, 16, 1.0, diag=True)
    cp(vw("BS", B_SUM, slice(15, 143, 16)), vw("L3", slice(8 * M_ONE, 8 * M_ONE + 8), 0))
    cp(c("LM", 128 * M_I, 128 * M_END), vw("L3", slice(8 * M_I, 8 * M_END)))
    ts(mat(M_HALF), mat(M_I), 0.5, ALU.mult)
    iota(c("pi", 0, 1), [[0, 1]], 0, 1)
    ts(c("pi", 1, 2), c("pi", 0, 1), 15, ALU.bitwise_and)
    cp(PM, c("pi", 1, 2))
    iota(c("vl"), [[16, 224]], 0, 0)
    iota(c("cw"), [[1, 224]], 0, 0)
    iota(c("cb", 0, 29), [[-1, 29]], 15, 0)
    ts(c("cb", 0, 29), c("cb", 0, 29), 0.0, ALU.min, 1.0 / 256, ALU.mult)
    ts(c("jl"), c("vl", 0, 48), PM, ALU.add)
    ts(c("vl"), c("vl"), PM, ALU.add, float(-W), ALU.add)
    ts(c("trl"), c("jl"), float(TR), ALU.add)
    ts(c("trm"), c("jl"), float(TR - 8192), ALU.add)
    ts(OHD, PM, float(EE), ALU.is_equal)
    ts(c("col", 3, 4), PM, float(V), ALU.add)
    ts(c("col", 4, 5), PM, 236.0, ALU.mult)
    ts(c("col", 5, 6), PM, 240.0, ALU.mult, float(UB), ALU.add)
    ts(c("col", 6, 7), PM, float(RG), ALU.is_equal)
    ms(c("one"), 1.0)
    ms(c("ZZ", 0, 240), 0.0)
    iota(c("jw"), [[1, L]], 0, 0)
    cp(c("barf", 0, 2), c("br"))
    ts(c("barf", 2, 3), c("barf", 1, 2), -1.0, ALU.mult, 1.0, ALU.add)
    ts(c("barf", 3, 4), c("barf", 1, 2), -1.0, ALU.mult, -2047.0, ALU.add)
    for r in range(RO):
        ms(c("X%d" % r, W, TR), 0.0)

    ts(c("n0", 0, 224), c("hg"), 1, ALU.arith_shift_right)
    cp(c("go"), c("n0", 0, 224))
    ts(c("n1", 0, 224), c("n0", 0, 224), 4095 - 31, ALU.bitwise_and)
    cp(c("at", 0, 224), c("n1", 0, 224))
    ts(c("n2", 0, 224), c("n0", 0, 224), 31, ALU.bitwise_and)
    cp(c("at", 224, 448), c("n2", 0, 224))
    ts(c("n3", 0, 224), c("hg"), 1, ALU.bitwise_and)
    ts(c("at", 448, 672), c("n3", 0, 224), 0.5, ALU.is_lt)
    ts(c("at", 672, 896), c("kd"), W - 0.5, ALU.is_lt)
    for i in range(16):
        o = c(P[i % 4], 0, 224)
        mm([(o, vw("SE", i, slice(15 - a, 143 - a)), c("at", 224 * k, 224 * k + 224)) for k, a in enumerate((AH, AL, NT, HS))])
        cp(c("B0", i, V, 16), o, "a")

    iota(c("n4"), [[1, 240]], 0, 0)
    ts(c("n1"), c("n4"), c("col", 4, 5), ALU.add)
    ts(c("n2"), c("n1"), 4095 - 31, ALU.bitwise_and)
    cp(c("idg", 0, 240), c("n2"))
    ts(c("n3"), c("n1"), 31, ALU.bitwise_and)
    cp(c("idg", 240, 480), c("n3"))
    ts(c("n1"), c("n4"), c("col", 5, 6), ALU.add)
    ts(c("n2"), c("n1"), 16383 - 63, ALU.bitwise_and)
    cp(c("sdg", 0, 240), c("n2"))
    ts(c("n3"), c("n1"), 63, ALU.bitwise_and)
    cp(c("sdg", 240, 480), c("n3"))
    ms(c("sdg", 480, 720), 8192.0)
    for a in range(0, W, 944):
        ms(c("B0", W + a, W + a + 944), 0.0)
    for a in range(0, 5 * L, 960):
        ms(c("SC", a, a + 960), 0.0)
    for rr, k in ((AH, 0), (AL, 1), (SH, 0), (SL, 1)):
        dma(row("B0", rr, W, W), c("idg", 240 * k, 240 * k + 236), 60e3)
    for rr, k in ((SH, 0), (SL, 1), (RG, 2)):
        dma(row("SC", rr, 0, 5 * L), c("sdg", 240 * k, 240 * k + 240), 60e3)
    for r in range(RO):
        ts(c("B%d" % r, V, W), c("B0", W + V, 2 * W), OHD, ALU.add)
    for r in range(1, RO):
        dma(c("B%d" % r, W, 2 * W), c("B0", W, 2 * W), 967e3)
    dma(row("B0", HS, W, V), row("B0", HS, 0, V), 60e3)

    def bent(r, a, b, val, s=None):
        o = vw("BS", slice(a, b, s), slice(15, 143, 16))
        asel(o, [[0, o["e"] // 8], [-16, 8]], ALU.not_equal, val, -r, 1)

    for r in (AH, AL):
        bent(r, B_PAR, B_OFF + 1, 1.0)
    for r in (CH, CL):
        bent(r, B_PAR, B_YH + 1, -1.0)
    for r in (DH, DL):
        bent(r, B_PAR, B_YH + 1, 1.0)
    bent(NT, B_IDX, B_OFF + 1, -8192.0, 2)
    bent(FL, B_IDX, B_IDX + 1, 8192.0)
    for r in (EH, EL):
        bent(r, B_ANC, B_ANC + 1, 1.0)
    for a in (AH, EH):
        ent(M_G, AH, a, a + 2, 1.0, diag=True)
        ent(M_G, CH, a, a + 2, -1.0, diag=True)
        ent(M_G, DH, a, a + 2, 1.0, diag=True)
    ent(M_G, NT, AH, FL + 1, M)
    ent(M_G, FL, AH, FL + 1, -M)
    ent(M_G, HS, FL, EE + 1, 1.0, EE - FL)
    ent(M_H, EE, AH, FL + 1, -M)
    ent(M_H, AC, AH, FL + 1, -M)
    ent(M_C, 0, CH, DH + 1, 16.0, DH - CH)
    cp(m3(M_M, CL, DL + 1, DL - CL), m3(M_ONE, 0, 2))
    ent(M_R, NT, AH, EE + 1, M)
    ent(M_R, DH, CH, CL + 1, 1.0, diag=True)
    ent(M_R, DH, DH, DL + 1, 1.0, diag=True)
    ent(M_R, FL, HS, HS + 1, 1.0)
    ent(M_R, AC, AC, AC + 1, 1.0)
    ent(M_R, EE, AC, AC + 1, 1.0)
    ent(M_R, FL, AC, AC + 1, -1.0)
    ent(M_R, EH, SH, SL + 1, 1.0, diag=True)
    ent(M_R, SH, SH, SL + 1, 1.0, diag=True)
    ent(M_R, AH, SH, SL + 1, -1.0, diag=True)
    ent(M_F, AC, HS, HS + 1, 1.0)
    ent(M_F, EE, HS, HS + 1, 1.0)
    ent(M_F, FL, HS, HS + 1, -1.0)
    cp(c("LM", 0, 128 * M_I), vw("L3", slice(0, 8 * M_I)), "va")
    ts(c("bias", 3, 4), PM, FL + 0.5, ALU.is_lt, -M, ALU.mult)
    ts(c("bias", 4, 5), PM, EE + 0.5, ALU.is_lt, -M, ALU.mult)
    ts(c("bias", 5, 6), PM, float(NT), ALU.is_equal)
    tt(c("bias", 0, 1), c("bias", 3, 4), c("bias", 5, 6), ALU.add)
    tt(c("bias", 1, 2), c("bias", 0, 1), c("bias", 4, 5), ALU.add)
    tt(c("bias", 2, 3), c("bias", 1, 2), c("bias", 3, 4), ALU.add)
    for r in (SH, SL):
        bent(r, B_ANC, B_SRC + 1, 1.0)
    bent(NT, B_YH, B_YH + 1, -0.5)
    bent(FL, B_FLP, B_FLP + 1, 0.5)

    CAND = c("ZZ", 240, 464)
    fsum = base(B_SUM)

    def compact(n, bk, parts):
        k = n // 16
        iota(c("CT", 0, n), [[0, n]], 0, 0)
        for (a, b, mark), bank in zip(parts, (bk[1], bk[2])):
            mark(c("ZZ", 240 + 16 * a, 240 + 16 * b), 16 * a, 16 * b)
            scan(c("ZZ", 16 * a + 1, 16 * b + 1), c("one", 16 * a, 16 * b), c("ZZ", 240 + 16 * a, 240 + 16 * b), ALU.mult, ALU.add,
                 c("ZZ", 16 * a, 16 * a + 1))
            o = c(bank, 0, 15 + b - a)
            mm([(o, mat(M_I), c("cb", a, 15 + b))] + tolist(o, fsum, "ZZ", 16 * a, 240 + 16 * (b - a)))
            ts(c("t6", a, b), c(bank, 15, 15 + b - a), -M, ALU.mult, c("col", 3, 4), ALU.add)
            tt(c("t7", a, b), c(bank, 0, b - a), c("t6", a, b), ALU.max)
            cp(c("co", a, b), c("t7", a, b))
            cp(ind(c("CT"), c("co", a, b)), c("cw", 16 * a, 16 * b))
        o2, o3 = c(bk[0], 0, 224), c(bk[0], 256, 257)
        mm([(o2, mat(M_ONE), c("ZZ", 0, 224)), (o2, mat(M_TRI), CAND), (o3, mat(M_ONE), c("ZZ", 224, 225))])
        cp(c("RT"), o2, "a")
        cp(TOT, o3, "a")
        scan(c("CW", 0, n), c("CT", 0, n), c("CT", 0, n), ALU.max, ALU.max)
        o4, o5 = c(bk[2], 0, k), c(bk[3], 0, k)
        mm(tolist(o4, fsum, "CW", 0, n))
        ts(c("cl", 0, k), o4, 1.0 / 16, ALU.mult)
        ts(c("iv", 0, k), c("jl", 0, k), TOT, ALU.is_ge, 8192.0, ALU.mult)
        mm(tolist(o5, fsum, "CW", 0, n) + [(o5, mat(M_I), c("iv", 0, k))], stop=False)
        tt(c("CM", 0, n), ind(c("RT"), c("cl", 0, k)), c("jw", 0, n), ALU.is_le)
        mm(tolist(o5, fsum, "CM", 0, n), start=False)
        return o5

    o = compact(192, [P[4], P[5], P[6], P[7]], [(0, 14, lambda z, a, b: ts(z, c("n0", a, b), V - 0.5, ALU.is_ge))])
    ts(c("se", 12, 24), o, float(V), ALU.min)
    cp(c("t8", 0, 12), c("iv", 0, 12))
    cp(c("EG"), ind(c("B0", 0, W), c("se", 12, 24)), "va")
    o = c(P[6], 0, 12)
    mm(tolist(o, base(B_PAR), "EG", 0, 192))
    ts(c("t9", 0, 12), o, float(-V), ALU.add, 0.0, ALU.max)
    tt(c("t9", 12, 24), c("t9", 0, 12), c("t8", 0, 12), ALU.add)
    ts(c("t9", 24, 36), c("jl", 0, 12), 192.0, ALU.add)
    tt(c("t9", 36, 48), c("t9", 12, 24), c("t9", 24, 36), ALU.min)
    cp(c("fp"), c("t9", 36, 48))
    cp(c("EG"), ind(c("B0", W, 2 * W), c("se", 12, 24)), "va")
    cp(c("SQ", 0, 192), c("B0", W + V, 2 * W), "va")
    cp(ind(c("SQ"), c("fp")), c("EG"))
    o = c(P[7], 0, 12)
    mm(tolist(o, base(B_SRC), "SQ", 0, 192))
    cp(c("se", 12, 24), o)

    CK = [(0, 896), (896, 896), (1792, 896), (2688, 896)]
    GK = [(0, 1120), (1120, 1120), (2240, 832), (3072, 512)]
    HK = [(448 * k, 448) for k in range(8)]
    for r in range(RO):
        X, B = "X%d" % r, "B%d" % r
        last = r == RO - 1
        o = c(P[6], 0, 224)
        for k in range(4):
            mm(tochunk(o, fsum, X, 0, range(4 * k, 4 * k + 4)), start=k == 0, stop=k == 3)
        addc(c("HV"), o, c("barf", 2, 3) if r == 0 else c("barf", 3, 4), relu=True)
        dma(row(B, AC, 0, V), c("HV"), 60e3)
        for k, (a, n) in enumerate(GK):
            tt(c("DD", a, a + n), ind(c(X, 0, W), c("go", a // 16, (a + n) // 16)), c("XC", a, a + n), ALU.subtract)
            x, o = c("DD", a, a + n), c("AB", a, a + n)
            add({"a": (acost(o, x), lambda g, o=o, x=x: g.scalar.activation(ap(o), ap(x), AF.Abs))}, [o], [x])
            mm(tolist(c(P[4 - k // 3], a // 16, (a + n) // 16), fsum, "AB", a, n))
            mm(tochunk(c(P[5], 0, 224), fsum, "AB", 0, range(a // 224, (a + n) // 224)), start=k == 0, stop=k == 3)
        if r == 0:
            for a in range(0, W, 944):
                addc(c(X, a, a + 944), c(X, a, a + 944), 128.0)
        o = compact(L, [P[0], P[1], P[6], P[2]], [(0, 12, lambda z, a, b: ts(z, c(P[4], a, b), TH, ALU.is_ge)),
                                                  (12, 14, lambda z, a, b: ts(z, c(P[3], a, b), TH, ALU.is_ge))])
        ts(c("dk", 0, 48), o, float(V), ALU.min)
        tt(c("t5"), o, c("trl"), ALU.min)
        cp(c("of", 0, 48), c("t5"))
        ts(c("CC"), c(P[5], 0, 224), TH, ALU.is_ge)
        scan(c("CS"), c("one"), c("CC"), ALU.mult, ALU.add)
        mm([(c(P[4], 0, 1), mat(M_STRI), c("CS", 223, 224))])
        ts(c("DT"), c("CS"), c(P[4], 0, 1), ALU.add, L + 0.5, ALU.is_lt)
        tt(c("DR"), c("DT"), c("CC"), ALU.mult)
        dma(row(B, EE, 0, V), c("DR"), 60e3)

        def half(name, k, h):
            return c(name, L * k + 384 * h, L * k + 384 * h + 384)

        def wide(bank, terms):
            os_ = [c(P[bank], 0, 384), c(P[bank + 1], 0, 384)]
            for h in range(2):
                for t, (m, nm, k) in enumerate(terms):
                    mm([(os_[h], mat(m), half(nm, k, h))], start=t == 0, stop=t == len(terms) - 1)
            return os_

        def scatter(k, src):
            n = 384 if k == 4 or k == 0 and not last else 192
            for a in range(0, L, n):
                tt(ind(c(B, W, BW), c("of", 48 * k + a // 16, 48 * k + (a + n) // 16)), c("RC", L * src + a, L * src + a + n),
                   c("SC", L * k + a, L * k + a + n), ALU.add)

        def record(k):
            if k == 0:
                terms = [(M_C, "CW", 0), (M_M, "CM", 0), (M_G, "GK", 0), (M_H, "GK", 1)]
            else:
                terms = [(M_G, "GK", k), (M_R, "RC", k - 1)] + ([(M_H, "GK", k + 1)] if k < 4 else [])
            os_ = wide(2 * (k % 2), terms)
            b = min(k, 1) + k // 4
            for h in range(2):
                addc(half("RC", k, h), os_[h], c("bias", b, b + 1), relu=True)
            if k < 4:
                o = c(P[6], 0, 48)
                mm(tolist(o, base(B_OFF), "RC", L * k, L))
                tt(c("t1"), o, c("trm"), ALU.min)
                ts(c("of", 48 * k + 48, 48 * k + 96), c("t1"), 8192.0, ALU.add)
            if k or last:
                scatter(k, k)
            if k:
                o = c(P[7], 0, 48)
                mm(tolist(o, base(B_ANC), "RC", L * k, L))
                cp(c("an", 48 * k - 48, 48 * k), o)

        for k in range(5):
            for h in range(2):
                cp(half("GK", k, h), ind(c(B, 0, W), c("dk", 48 * k + 24 * h, 48 * k + 24 * h + 24)), "va")
            if k < 4:
                o = c(P[4 + k % 2], 0, 48)
                mm(tolist(o, base(B_PAR), "GK", L * k, L))
                cp(c("dk", 48 * k + 48, 48 * k + 96), o)
            if k:
                record(k - 1)
        record(4)
        if not last:
            os_ = wide(2, [(M_I, "RC", 0), (M_F, "RC", 4)])
            for h in range(2):
                cp(half("RC", 5, h), os_[h], "va")
            scatter(0, 5)
        for a, n in CK:
            mm(tolist(c(P[5], a // 16, (a + n) // 16), base(B_IDX), B, a, n))
        tt(c("t0"), c(P[5], 0, 224), c("vl"), ALU.max)
        ts(c("ix"), c("t0"), float(W), ALU.add)
        for k in range(6):
            for h in range(2):
                a = 24 * h
                cp(half("NG", k, h),
                   ind(c(X, 0, W), c("dk", 48 * k + a, 48 * k + a + 24) if k < 2 else c("an", 48 * k - 96 + a, 48 * k - 72 + a)), "va")
        for k in range(4, -1, -1):
            un, up = ("NG", 5 * L) if k == 4 else (X, UB + L * (k + 1))
            for h in range(2):
                a = 384 * h
                o = c(P[2 * (k % 2) + h], 0, 384)
                mm([(o, mat(M_HALF), half("NG", k, h)), (o, mat(M_HALF), c(un, up + a, up + a + 384))])
                addc(c(X, UB + L * k + a, UB + L * k + a + 384), o, -0.125)
        if not last:
            Xn, Bn, MS, LD = "X%d" % (r + 1), "B%d" % (r + 1), "MS%d" % (r + 1), "LD%d" % (r + 1)
            cp(c("SQ", 0, 192), ind(c(B, W, 2 * W), c("se", 0, 12)), "va")
            o = c(P[6], 0, 12)
            mm(tolist(o, base(B_SRC), "SQ", 0, 192))
            for d in range(3):
                ts(c(MS, 128 * d + G, 128 * d + 128), ind(c(B, W, 2 * W), c("se", 20 - 4 * d, 24 - 4 * d)), c("col", 6, 7), ALU.mult)
            cp(c("ss"), o)
            for d in range(3):
                cp(c(MS, 128 * d, 128 * d + G), ind(c(X), c("ss", 4 * d, 4 * d + 4)), "va")
            exchange(r + 1, MS, (LD, 0), 128)
        for k, (a, n) in enumerate(CK):
            o = c(P[4 + k % 2], 0, n // 16)
            mm(tolist(o, base(B_SRC), B, W + a, n))
            cp(c("sr", a // 16, (a + n) // 16), o)
        Pn = "PF" if last else Bn
        for a, n in HK:
            cp(c(Pn, a, a + n), ind(c(B, 0, 2 * W), c("ix", a // 16, (a + n) // 16)), "va")
        if last:
            o = c(P[6], 0, 224)
            mm(tochunk(o, base(B_FLP), B, W), stop=False)
            for k in range(4):
                mm(tochunk(o, base(B_YH), Pn, 0, range(4 * k, 4 * k + 4)), start=False, stop=k == 3)
            ts(c("yo"), o, 2.0, ALU.mult, 1.0, ALU.add)
            dma(vw("yh"), c("yo"), 115e3)
            for k, (a, n) in enumerate(HK):
                addc(c("AB", a, a + n), ind(c(X), c("sr", a // 16, (a + n) // 16)), -128.0)
                if k % 2:
                    dma(vw("y", slice(None), slice(a - n, a + n)), c("AB", a - n, a + n), 230e3)
        else:
            for a, n in HK:
                cp(c(Xn, a, a + n), ind(c(X), c("sr", a // 16, (a + n) // 16)), "va")
                cp(c("XC", a, a + n), c(Xn, a, a + n), "g" if a < 2 * n else "va")
            for d in range(3):
                cp(c(Xn, V + G * d, V + G * d + G), c(LD, 128 * d, 128 * d + G), "va")
            for d in range(3):
                tt(ind(c("XC"), c("se", 4 * d, 4 * d + 4)), c(MS, 128 * d, 128 * d + G),
                   c(LD, 128 * (2 - d) + G, 128 * (2 - d) + 128), ALU.add)
            for k, (a, n) in enumerate(GK):
                o = c(P[k], 0, n // 16)
                mm(tolist(o, base(B_PAR), Bn, a, n))
                cp(c("go", a // 16, (a + n) // 16), o)
            dma(row(Bn, FL, 0, V), row(B, FL, W, V), 60e3)
            dma(row(Bn, HS, 0, V), row(B, HS, W, V), 60e3)
            dma(row(Bn, HS, W, V), row(B, HS, W, V), 60e3)
    return ops


def link(ops):
    hist = {}
    deps = []
    for k, o in enumerate(ops):
        d = {q: "x" for q in o.get("after", [])}
        accs = [(x, False) for x in o["r"]] + [(x, True) for x in o["w"]]
        for acc, wr in accs:
            psum = acc["n"].startswith("ps")
            for q, y, w2 in hist.get(acc["n"], []):
                lo, hi, l2, h2 = acc["lo"], acc["hi"], y["lo"], y["hi"]
                if wr and w2:
                    u = 16 // acc["w"]
                    lo, hi, l2, h2 = lo // u * u, -(-hi // u) * u, l2 // u * u, -(-h2 // u) * u
                real = (wr or w2) and lo < h2 and l2 < hi and acc["pm"] & y["pm"]
                if real and not (psum and wr and w2 and "p" in o["alts"] and "p" in ops[q]["alts"]):
                    d[q] = "x"
                elif psum:
                    d.setdefault(q, "o")
        for acc, wr in accs:
            h = hist.setdefault(acc["n"], [])
            if acc["n"].startswith("ps"):
                del h[:-30]
            elif wr:
                h[:] = [z for z in h if not (acc["lo"] <= z[1]["lo"] and z[1]["hi"] <= acc["hi"] and z[1]["pm"] & ~acc["pm"] == 0
                                             and z[0] in d)]
            if not h or h[-1][0] != k or h[-1][1] is not acc or h[-1][2] != wr:
                h.append((k, acc, wr))
        deps.append(d)
    return deps


def place(alts, lat, pred, order):
    n = len(alts)
    begin, end = {e: [] for e in "vapgsn"}, {e: [] for e in "vapgsn"}
    fin, eng, start = [0.0] * n, [None] * n, [0.0] * n
    for k in order:
        best = None
        for e, cost in alts[k]:
            s = 0.0
            for q in pred[k]:
                t = fin[q] + (SAME if eng[q] == e else CROSS)
                if t > s:
                    s = t
            bg, en = begin[e], end[e]
            lo, hi = 0, len(en)
            while lo < hi:
                mid = (lo + hi) // 2
                if en[mid] > s:
                    hi = mid
                else:
                    lo = mid + 1
            while lo < len(en) and s + cost > bg[lo]:
                s = en[lo]
                lo += 1
            if best is None or s + cost < best[0]:
                best = (s + cost, s, e, lo)
        f, s, e, lo = best
        eng[k], start[k], fin[k] = e, s, f + lat[k]
        begin[e].insert(lo, s)
        end[e].insert(lo, f)
    return eng, start, fin


def plan(ops, deps, passes=PASSES, first=BONUS, seed=5):
    n = len(ops)
    pred = []
    for k in range(n):
        pred.append([q for q in deps[k] if not any(q in deps[z] for z in deps[k])])
    succ = [[] for _ in range(n)]
    for k in range(n):
        for q in pred[k]:
            succ[q].append(k)
    alts = [[(e, a[0]) for e, a in o["alts"].items()] for o in ops]
    lat = [o.get("lat", 0) for o in ops]
    own = [min(a[1] for a in alts[k]) + lat[k] + 100 for k in range(n)]
    rng = np.random.default_rng(seed)
    names = {}
    tag = [names.setdefault((o["w"][0]["n"].rstrip("012"), o["w"][0]["lo"], o["r"][0]["n"].rstrip("012") if o["r"] else 0,
                             o["r"][0]["lo"] if o["r"] else 0, 4 * k > 3 * n + 40) if o["w"] else k, len(names))
           for k, o in enumerate(ops)]
    best, bonus = None, [100.0 * first.get(t, 0) for t in range(len(names))]
    late = crit = None
    for t in range(passes):
        trial = list(bonus)
        if t:
            for k in [late[rng.integers(len(late))], crit[rng.integers(len(crit))]][rng.integers(2):]:
                trial[tag[k]] = max(0.0, 100.0 * round(trial[tag[k]] / 100 + rng.normal() * (4, 25)[rng.integers(2)]))
        key = [0.0] * n
        for k in range(n - 1, -1, -1):
            key[k] = own[k] + trial[tag[k]] + max([key[s] for s in succ[k]], default=0)
        z = place(alts, lat, pred, sorted(range(n), key=lambda k: (-key[k], k)))
        if best is None or max(z[2]) <= best[0]:
            best, bonus = (max(z[2]), z), trial
            late = [k for k in range(n) if z[1][k] > 150 + max([z[2][q] for q in pred[k]], default=0)]
            before, prev = {}, {}
            for k in sorted(range(n), key=lambda k: z[1][k]):
                before[k], prev[z[0][k]] = prev.get(z[0][k]), k
            crit, k = [], max(range(n), key=lambda k: z[2][k])
            while k is not None:
                q = max(pred[k], key=lambda q: z[2][q], default=None)
                if before[k] is not None and (q is None or z[1][k] > z[2][q] + CROSS + 1):
                    q = before[k]
                    crit += [k, q]
                k = q
    eng, start, fin = best[1]
    _plan["bonus"] = {t: int(b / 100) for t, b in enumerate(bonus) if b}
    return sorted(range(n), key=lambda k: (start[k], k)), eng, start, fin


def rank_program(g, core, T, topo):
    rank = T.rank_of(core)
    if rank is None:
        return
    ops = build(rank, T, topo)
    if "deps" not in _plan:
        _plan["deps"] = link(ops)
        _plan["plan"] = plan(ops, _plan["deps"])
    deps = _plan["deps"]
    order, eng, start, fin = _plan["plan"]
    queue = {"v": g.vector, "a": g.scalar, "p": g.tensor, "g": g, "s": g.sync}
    count = {e: 0 for e in "vapg"}
    known = {e: {} for e in queue}
    token, clock, ndma = {}, {}, 0
    for k in order:
        o, e = ops[k], eng[k]
        if o["kind"] == "recv":
            token[k], clock[k] = o["sem"], {}
            continue
        need = {}
        for q, how in deps[k].items():
            if how == "o" and eng[q] == e:
                continue
            s, val = token[q]
            need[s] = max(need.get(s, (0, 0)), (val, q))
        kn = known[e]
        for s, (val, q) in sorted(need.items(), key=lambda z: -fin[z[1][1]]):
            if kn.get(s, 0) < val:
                queue[e].wait_ge(T.sem[s], val)
                kn[s] = val
                for s2, v2 in clock[q].items():
                    kn[s2] = max(kn.get(s2, 0), v2)
        ins = o["alts"][e][1](g)
        if o["kind"] == "dma":
            token[k] = ("d%d" % ndma, 16)
            ins.then_inc(T.sem[token[k][0]], 16)
            ndma += 1
        elif o["kind"] == "send":
            token[k] = o["sem"]
        else:
            count[e] += 1
            token[k] = (e, count[e])
            ins.then_inc(T.sem[e], 1)
        clock[k] = dict(kn)
    final = {}
    for s, val in token.values():
        final[s] = max(final.get(s, 0), val)
    for s, val in final.items():
        if known["g"].get(s, 0) < val:
            g.wait_ge(T.sem[s], val)
